import numpy as np
import ml_dtypes


def mxq(x, axis, fmt="e4m3"):
    dtype, down = {"e4m3": (ml_dtypes.float8_e4m3fn, 7), "e5m2": (ml_dtypes.float8_e5m2, 14)}[fmt]
    v = np.moveaxis(np.asarray(x, np.float32).astype(ml_dtypes.bfloat16).astype(np.float64), axis, -1)
    blocks = v.reshape(v.shape[:-1] + (-1, 32))
    amax = np.abs(blocks).max(-1, keepdims=True)
    byte = np.maximum(np.where(amax > 0, np.frexp(amax)[1] - 1 + 127, 0) - down, 1)
    scale = np.exp2(byte - 127.0)
    codes = (blocks / scale).astype(np.float32).astype(dtype).astype(np.float64)
    return np.moveaxis((codes * scale).reshape(v.shape), -1, axis)


WIDE = False


def mx_kscale(k):
    if not WIDE:
        return np.ones(k)
    levels = np.array([10, -10, 5, -5, 0])
    if k % 512:
        return np.exp2(np.random.permutation(np.resize(levels, k // 32))).repeat(32)
    a = np.empty((k // 512, 16))
    for p in range(k // 512):
        a[p, :8] = np.random.permutation(np.resize(levels, 8))
        for g in range(8):
            far = levels[np.abs(levels - a[p, g]) >= 10]
            a[p, g + 8] = far[np.random.randint(len(far))]
    return np.exp2(a.ravel()).repeat(32)


def f64(x):
    return np.asarray(x).astype(np.float64)


def striped(idx):
    return np.tile(idx.reshape(-1, 16).T, (8, 1)).astype(np.uint16)


def unstriped(offs):
    return offs[:16].T.reshape(-1).astype(np.int64)


def pack_weight(w):
    k, n = w.shape
    w = f64(np.asarray(w, np.float32).astype(ml_dtypes.bfloat16)).reshape(k // 32, 32, n)
    amax = np.abs(w).max(1)
    byte = np.clip(np.where(amax > 0, np.frexp(amax)[1] - 1 + 127 - 7, 1), 1, 254)
    scaled = (w * np.exp2(127.0 - byte)[:, None, :]).reshape(k, n).astype(np.float32)
    words = np.ascontiguousarray(scaled.reshape(k // 512, 128, 4, n).transpose(0, 1, 3, 2)).astype(ml_dtypes.float8_e4m3fn).view(np.uint8)
    return words, np.ascontiguousarray(byte.astype(np.uint8).reshape(k // 512, 16, n))


def unpack_weight(words, scales):
    g, p, n, _ = words.shape
    vals = np.ascontiguousarray(words).view(ml_dtypes.float8_e4m3fn).astype(np.float64) * np.repeat(np.exp2(scales.astype(np.float64) - 127.0), 8, axis=1)[..., None]
    return vals.transpose(0, 1, 3, 2).reshape(g * 512, n)


def planes(y):
    n, m = y.shape
    v = y.astype(np.float32).astype(ml_dtypes.bfloat16).astype(np.float64).reshape(n // 32, 32, m)
    top = np.abs(v).max(1)
    byte = np.clip(np.where(top > 0, np.frexp(top)[1] - 1 + 127 - 7, 1), 1, 254)
    codes = (v * np.exp2(127.0 - byte)[:, None, :]).reshape(n, m).astype(np.float32).astype(ml_dtypes.float8_e4m3fn).view(np.uint8)
    words = codes.reshape(n // 512, 128, 4, m).transpose(0, 1, 3, 2)
    return np.ascontiguousarray(words), np.ascontiguousarray(byte.astype(np.uint8).reshape(n // 512, 16, m))


K, T, S, D, V, H, N = 512, 4096, 1024, 4, 256, 512, 512


def setup_inputs():
    n = np.random.standard_normal
    s = mx_kscale(K)[:, None]
    u = mx_kscale(H)
    packed_xT = pack_weight(n((K, T)) * s)
    packed_w2 = pack_weight(n((K, N)) / np.sqrt(K) / s)
    packed_w3 = pack_weight(n((H, N)) / np.sqrt(H) / u[:, None])
    return {
        "x_words": packed_xT[0],
        "x_scales": packed_xT[1],
        "w1": (n((K, H)) / np.sqrt(K) / s * u).astype(np.float32),
        "w2_words": packed_w2[0],
        "w2_scales": packed_w2[1],
        "w3_words": packed_w3[0],
        "w3_scales": packed_w3[1],
        "offs": striped(np.random.permutation(T)[:S]),
    }


def reference(x_words, x_scales, w1, w2_words, w2_scales, w3_words, w3_scales, offs):
    xq = unpack_weight(x_words, x_scales)[:, unstriped(offs)]
    h = mxq(f64(w1), 0, "e4m3").T @ xq
    sh = h.reshape(H, V, D).sum(axis=2)
    e = unpack_weight(w2_words, w2_scales).T @ xq
    se = e.reshape(H, V, D).sum(axis=2)
    z = sh * se - ((h * e).reshape(H, V, D).sum(axis=2))
    zm = z / 12
    out_0 = unpack_weight(w3_words, w3_scales).T @ mxq(zm, 0, "e4m3")
    return (out_0,) + planes(out_0)

@@ -1,0 +1,217 @@
+from contextlib import ExitStack
+
+import concourse.mybir as mybir
+from concourse.masks import make_identity
+
+K, T, S, D, V, H, N = 512, 4096, 1024, 4, 256, 512, 512
+FLOPS = 2 * (2 * K * H * S) + 2 * H * N * V
+
+F32 = mybir.dt.float32
+BF16 = mybir.dt.bfloat16
+I32 = mybir.dt.int32
+U32 = mybir.dt.uint32
+U16 = mybir.dt.uint16
+U8 = mybir.dt.uint8
+FP8X4 = mybir.dt.float8_e4m3fn_x4
+ADD = mybir.AluOpType.add
+SUB = mybir.AluOpType.subtract
+MULT = mybir.AluOpType.mult
+COPY = mybir.ActivationFunctionType.Copy
+
+P = 128
+PACK = 4
+REC = 128
+HH = H // 2
+MH = HH // PACK
+W2_ROW = 4
+W3_ROW = 8
+
+
+def load_scale_rows(queue, plane, scales, first_row):
+    for q in range(4):
+        queue.dma_start(
+            out=plane[32 * q + first_row : 32 * q + first_row + 4, :].bitcast(I32),
+            in_=scales[0, 4 * q : 4 * q + 4, :].bitcast(I32),
+        )
+
+
+def words_of(dram):
+    return dram[0].rearrange("p n t -> p (n t)").bitcast(I32)
+
+
+def tile_picked_zfm_mean_po_kernel(
+    tc, x_words, x_scales, w1, w2_words, w2_scales, w3_words, w3_scales, offs, out_0, out_1, out_2
+):
+    nc = tc.nc
+    with ExitStack() as ctx:
+        keep = ctx.enter_context(tc.tile_pool(name="keep", bufs=1))
+        reuse = ctx.enter_context(tc.tile_pool(name="reuse", bufs=1))
+        work = ctx.enter_context(tc.tile_pool(name="work", bufs=2))
+        psum = ctx.enter_context(tc.psum_pool(name="psum", bufs=1))
+
+        offsets = keep.tile([P, S // 16], U16, name="offsets")
+        nc.sync.dma_start(offsets[:], offs)
+        x_table = reuse.tile([P, T], U32, name="x_table", align_bytes=64, offset=0)
+        nc.sync.dma_start(out=x_table[:].bitcast(I32), in_=words_of(x_words))
+
+        xs_table = reuse.tile([P, T], U8, name="xs_table", align_bytes=64, offset=16384)
+        nc.vector.memset(xs_table[:].bitcast(I32), 0)
+        load_scale_rows(nc.scalar, xs_table, x_scales, 0)
+
+        w2_codes = keep.tile([P, H], U32, name="w2_codes", align_bytes=64)
+        nc.sync.dma_start(out=w2_codes[:].bitcast(I32), in_=words_of(w2_words))
+
+        def load_w1(ih, offset):
+            raw = reuse.tile([P, PACK, HH], F32, name=f"w1_raw{ih}", align_bytes=64, offset=offset)
+            nc.sync.dma_start(out=raw[:], in_=w1[:, ih * HH : (ih + 1) * HH].rearrange("(p j) c -> p j c", j=PACK))
+            return raw
+
+        w1_raw = [load_w1(0, 20480)]
+
+        w2_plane = keep.tile([P, H], U8, name="w2_plane", align_bytes=64)
+        nc.gpsimd.memset(w2_plane[:].bitcast(I32), 0)
+        load_scale_rows(nc.gpsimd, w2_plane, w2_scales, W2_ROW)
+        identity = keep.tile([P, P], F32, name="identity")
+        make_identity(nc, identity[:])
+
+        xs_picked = reuse.tile([P, S], U8, name="xs_picked", align_bytes=64, offset=24576)
+        nc.vector.tensor_copy(xs_picked[:], xs_table[:].indirect(offsets[:]))
+        w1_raw.append(load_w1(1, 16384))
+        x_plane = keep.tile([P, 2, D, REC], U8, name="x_plane", align_bytes=64)
+        nc.vector.tensor_copy(x_plane[:], xs_picked[:].rearrange("p (g v d) -> p g d v", g=2, d=D))
+
+        x_codes = []
+        for g in range(2):
+            codes = reuse.tile([P, D, REC], U32, name=f"x_codes{g}", align_bytes=64, offset=24576 + 512 + 2048 * g)
+            cols = REC * D // 16
+            nc.vector.tensor_copy(
+                codes[:].rearrange("p d v -> p v d"), x_table[:].indirect(offsets[:, g * cols : (g + 1) * cols])
+            )
+            x_codes.append(codes)
+
+        w1_codes, w1_plane = [], []
+
+        def quantise_w1(ih):
+            grouped = keep.tile([P, HH * PACK], BF16, name="w1_grouped", align_bytes=64)
+            nc.scalar.activation(
+                grouped[:].rearrange("p (m t j) -> p m j t", t=PACK, j=PACK),
+                w1_raw[ih][:].rearrange("p j (m t) -> p m j t", t=PACK),
+                COPY,
+            )
+            codes = reuse.tile([P, HH], U32, name=f"w1_codes{ih}", align_bytes=64, offset=1024 * ih)
+            plane = keep.tile([P, HH], U8, name=f"w1_plane{ih}", align_bytes=64)
+            nc.vector.quantize_mx(out=codes[:].bitcast(FP8X4), scales=plane[:], in_=grouped[:])
+            w1_codes.append(codes)
+            w1_plane.append(plane)
+
+        w3_codes = keep.tile([P, N], U32, name="w3_codes", align_bytes=64)
+        w3_plane = keep.tile([P, N], U8, name="w3_plane", align_bytes=64)
+
+        def load_w3():
+            raw = reuse.tile([P, N], U32, name="w3_raw", align_bytes=64, offset=20480)
+            nc.sync.dma_start(out=raw[:].bitcast(I32), in_=words_of(w3_words))
+            nc.gpsimd.tensor_copy(
+                w3_codes[:].rearrange("p (t m) -> p t m", t=PACK), raw[:].rearrange("p (m t) -> p t m", t=PACK)
+            )
+            plane_raw = reuse.tile([P, N], U8, name="w3_plane_raw", align_bytes=64, offset=2048)
+            nc.gpsimd.memset(plane_raw[:].bitcast(I32), 0)
+            load_scale_rows(nc.sync, plane_raw, w3_scales, W3_ROW)
+            nc.gpsimd.tensor_copy(
+                w3_plane[:].rearrange("p (t m) -> p t m", t=PACK), plane_raw[:].rearrange("p (m t) -> p t m", t=PACK)
+            )
+
+        y_codes = keep.tile([P, V], U32, name="y_codes", align_bytes=64)
+        y_plane = keep.tile([P, V], U8, name="y_plane", align_bytes=64)
+
+        def project(bank, g, fields, codes, plane):
+            for a, group in enumerate(fields):
+                for n, d in enumerate(group):
+                    nc.tensor.matmul_mx(
+                        out=bank[:, a * HH : (a + 1) * HH],
+                        lhsT=x_codes[g][:, d, :].bitcast(FP8X4),
+                        lhsT_scale=x_plane[:, g, d, :],
+                        rhs=codes.bitcast(FP8X4),
+                        rhs_scale=plane,
+                        start=(n == 0),
+                        stop=(n == len(group) - 1),
+                    )
+
+        def dealt(bank):
+            return bank[:].rearrange("p (a m t) -> p a t m", a=2, t=PACK)
+
+        def block(g, ih, terms):
+            cols = slice(ih * HH, (ih + 1) * HH)
+            e_even = psum.tile([P, 2 * HH], F32, name="e_even", bufs=1)
+            e_odd = psum.tile([P, 2 * HH], F32, name="e_odd", bufs=2)
+            h_single = psum.tile([P, 2 * HH], F32, name="h_single", bufs=2)
+            h_pair = psum.tile([P, 2 * HH], F32, name="h_pair", bufs=2)
+            project(e_even, g, [[0], [2]], w2_codes[:, cols], w2_plane[W2_ROW:, cols])
+            project(e_odd, g, [[1], [3]], w2_codes[:, cols], w2_plane[W2_ROW:, cols])
+            project(h_single, g, [[0], [2]], w1_codes[ih][:], w1_plane[ih][:])
+            project(h_pair, g, [[2, 3], [0, 1]], w1_codes[ih][:], w1_plane[ih][:])
+
+            even = work.tile([P, 2, PACK, MH], F32, name="even")
+            nc.scalar.activation(even[:], dealt(e_even), COPY)
+            even_sum = work.tile([P, 1, PACK, MH], F32, name="even_sum")
+            nc.gpsimd.tensor_tensor(even_sum[:], even[:, 0:1], even[:, 1:2], ADD)
+            diff = work.tile([P, 2, PACK, MH], F32, name="diff")
+            nc.vector.tensor_tensor(diff[:], dealt(e_odd), even[:], SUB)
+            trio = work.tile([P, 2, PACK, MH], F32, name="trio")
+            nc.vector.tensor_tensor(trio[:], dealt(e_odd), even_sum[:].to_broadcast([P, 2, PACK, MH]), ADD)
+            for a, (bank, factor) in enumerate(((h_single, diff), (h_pair, trio))):
+                nc.vector.tensor_tensor(
+                    terms[:, 2 * a : 2 * a + 2, :, ih * MH : (ih + 1) * MH], dealt(bank), factor[:], MULT
+                )
+
+        def finish(g, terms):
+            recs = slice(g * REC, (g + 1) * REC)
+            z = psum.tile([P, PACK, REC], F32, name="tail", bufs=1)
+            for t in range(PACK):
+                for a in range(4):
+                    nc.tensor.matmul(
+                        z[:, t, :], terms[:, a, t, :], identity[:], start=(a == 0), stop=(a == 3), is_transpose=True
+                    )
+            zm = work.tile([P, REC, PACK], BF16, name="zm", align_bytes=64)
+            nc.scalar.activation(zm[:], z[:].rearrange("p t v -> p v t"), COPY, scale=1.0 / 12.0)
+            zm_codes = work.tile([P, REC], U32, name="zm_codes", align_bytes=64)
+            zm_plane = work.tile([P, REC], U8, name="zm_plane", align_bytes=64)
+            nc.vector.quantize_mx(
+                out=zm_codes[:].bitcast(FP8X4), scales=zm_plane[:], in_=zm[:].rearrange("p v t -> p (v t)")
+            )
+            y = psum.tile([P, PACK, REC], F32, name="tail", bufs=1)
+            for t in range(PACK):
+                nc.tensor.matmul_mx(
+                    out=y[:, t, :],
+                    lhsT=w3_codes[:, t * P : (t + 1) * P].bitcast(FP8X4),
+                    lhsT_scale=w3_plane[W3_ROW:, t * P : (t + 1) * P],
+                    rhs=zm_codes[:].bitcast(FP8X4),
+                    rhs_scale=zm_plane[:],
+                    start=True,
+                    stop=True,
+                )
+            y_out = work.tile([P, PACK, REC], F32, name="y_out")
+            nc.scalar.copy(y_out[:], y[:])
+            nc.sync.dma_start(out=out_0.rearrange("(p t) v -> p t v", t=PACK)[:, :, recs], in_=y_out[:])
+            y_grouped = work.tile([P, REC, PACK], BF16, name="y_grouped", align_bytes=64)
+            nc.vector.tensor_copy(y_grouped[:], y_out[:].rearrange("p t v -> p v t"))
+            nc.vector.quantize_mx(
+                out=y_codes[:, recs].bitcast(FP8X4),
+                scales=y_plane[:, recs],
+                in_=y_grouped[:].rearrange("p v t -> p (v t)"),
+            )
+            nc.sync.dma_start(out=words_of(out_1)[:, recs], in_=y_codes[:, recs].bitcast(I32))
+
+        terms = [work.tile([P, 4, PACK, P], F32, name="terms") for g in range(2)]
+        quantise_w1(0)
+        block(0, 0, terms[0])
+        quantise_w1(1)
+        block(0, 1, terms[0])
+        load_w3()
+        block(1, 0, terms[1])
+        finish(0, terms[0])
+        block(1, 1, terms[1])
+        finish(1, terms[1])
+        for q in range(4):
+            nc.scalar.dma_start(
+                out=out_2[0, 4 * q : 4 * q + 4, :].bitcast(I32), in_=y_plane[32 * q : 32 * q + 4, :].bitcast(I32)
+            )

@@ -27,9 +27,9 @@ W2_ROW = 4
 W3_ROW = 8
 
 
-def load_scale_rows(queue, plane, scales, first_row):
+def load_scale_rows(queues, plane, scales, first_row):
     for q in range(4):
-        queue.dma_start(
+        queues[q % len(queues)].dma_start(
             out=plane[32 * q + first_row : 32 * q + first_row + 4, :].bitcast(I32),
             in_=scales[0, 4 * q : 4 * q + 4, :].bitcast(I32),
         )
@@ -49,40 +49,44 @@ def tile_picked_zfm_mean_po_kernel(
         work = ctx.enter_context(tc.tile_pool(name="work", bufs=2))
         psum = ctx.enter_context(tc.psum_pool(name="psum", bufs=1))
 
+        xs_table = keep.tile([P, T], U8, name="xs_table", align_bytes=64)
+        nc.sync.dma_start(out=xs_table[P - 16 :, :].bitcast(I32), in_=x_scales[0].bitcast(I32))
+        nc.vector.memset(xs_table[: P - 16, :].bitcast(I32), 0)
         offsets = keep.tile([P, S // 16], U16, name="offsets")
         nc.sync.dma_start(offsets[:], offs)
         x_table = reuse.tile([P, T], U32, name="x_table", align_bytes=64, offset=0)
         nc.sync.dma_start(out=x_table[:].bitcast(I32), in_=words_of(x_words))
-
-        xs_table = reuse.tile([P, T], U8, name="xs_table", align_bytes=64, offset=16384)
-        nc.vector.memset(xs_table[:].bitcast(I32), 0)
-        load_scale_rows(nc.scalar, xs_table, x_scales, 0)
-
-        w2_codes = keep.tile([P, H], U32, name="w2_codes", align_bytes=64)
-        nc.sync.dma_start(out=w2_codes[:].bitcast(I32), in_=words_of(w2_words))
 
         def load_w1(ih, offset):
             raw = reuse.tile([P, PACK, HH], F32, name=f"w1_raw{ih}", align_bytes=64, offset=offset)
             nc.sync.dma_start(out=raw[:], in_=w1[:, ih * HH : (ih + 1) * HH].rearrange("(p j) c -> p j c", j=PACK))
             return raw
 
-        w1_raw = [load_w1(0, 20480)]
+        w1_raw = [load_w1(0, 24576)]
+        w2_codes = keep.tile([P, H], U32, name="w2_codes", align_bytes=64)
+        nc.sync.dma_start(out=w2_codes[:].bitcast(I32), in_=words_of(w2_words))
+
 
         w2_plane = keep.tile([P, H], U8, name="w2_plane", align_bytes=64)
         nc.gpsimd.memset(w2_plane[:].bitcast(I32), 0)
-        load_scale_rows(nc.gpsimd, w2_plane, w2_scales, W2_ROW)
-        identity = keep.tile([P, P], F32, name="identity")
-        make_identity(nc, identity[:])
+        load_scale_rows([nc.gpsimd], w2_plane, w2_scales, W2_ROW)
 
-        xs_picked = reuse.tile([P, S], U8, name="xs_picked", align_bytes=64, offset=24576)
+        xs_picked = reuse.tile([P, S], U8, name="xs_picked", align_bytes=64, offset=20480 - 512)
         nc.vector.tensor_copy(xs_picked[:], xs_table[:].indirect(offsets[:]))
-        w1_raw.append(load_w1(1, 16384))
+        xs_sorted = keep.tile([P, 2, D, REC], U8, name="xs_sorted", align_bytes=64)
+        nc.vector.tensor_copy(xs_sorted[:], xs_picked[:].rearrange("p (g v d) -> p g d v", g=2, d=D))
         x_plane = keep.tile([P, 2, D, REC], U8, name="x_plane", align_bytes=64)
-        nc.vector.tensor_copy(x_plane[:], xs_picked[:].rearrange("p (g v d) -> p g d v", g=2, d=D))
+        nc.vector.memset(x_plane[:].bitcast(I32), 0)
+        for q in range(4):
+            nc.sync.dma_start(
+                out=x_plane[32 * q : 32 * q + 4].rearrange("p g d v -> p (g d v)").bitcast(I32),
+                in_=xs_sorted[P - 16 + 4 * q : P - 12 + 4 * q].rearrange("p g d v -> p (g d v)").bitcast(I32),
+            )
+        w1_raw.append(load_w1(1, 16384))
 
         x_codes = []
         for g in range(2):
-            codes = reuse.tile([P, D, REC], U32, name=f"x_codes{g}", align_bytes=64, offset=24576 + 512 + 2048 * g)
+            codes = keep.tile([P, D, REC], U32, name=f"x_codes{g}", align_bytes=64)
             cols = REC * D // 16
             nc.vector.tensor_copy(
                 codes[:].rearrange("p d v -> p v d"), x_table[:].indirect(offsets[:, g * cols : (g + 1) * cols])
@@ -108,18 +112,20 @@ def tile_picked_zfm_mean_po_kernel(
         w3_plane = keep.tile([P, N], U8, name="w3_plane", align_bytes=64)
 
         def load_w3():
-            raw = reuse.tile([P, N], U32, name="w3_raw", align_bytes=64, offset=20480)
+            raw = reuse.tile([P, N], U32, name="w3_raw", align_bytes=64, offset=24576)
             nc.sync.dma_start(out=raw[:].bitcast(I32), in_=words_of(w3_words))
             nc.gpsimd.tensor_copy(
                 w3_codes[:].rearrange("p (t m) -> p t m", t=PACK), raw[:].rearrange("p (m t) -> p t m", t=PACK)
             )
             plane_raw = reuse.tile([P, N], U8, name="w3_plane_raw", align_bytes=64, offset=2048)
             nc.gpsimd.memset(plane_raw[:].bitcast(I32), 0)
-            load_scale_rows(nc.sync, plane_raw, w3_scales, W3_ROW)
+            load_scale_rows([nc.sync], plane_raw, w3_scales, W3_ROW)
             nc.gpsimd.tensor_copy(
                 w3_plane[:].rearrange("p (t m) -> p t m", t=PACK), plane_raw[:].rearrange("p (m t) -> p t m", t=PACK)
             )
 
+        identity = reuse.tile([P, P], F32, name="identity", align_bytes=64, offset=20480)
+        make_identity(nc, identity[:])
         y_codes = keep.tile([P, V], U32, name="y_codes", align_bytes=64)
         y_plane = keep.tile([P, V], U8, name="y_plane", align_bytes=64)
 
@@ -163,16 +169,31 @@ def tile_picked_zfm_mean_po_kernel(
                     terms[:, 2 * a : 2 * a + 2, :, ih * MH : (ih + 1) * MH], dealt(bank), factor[:], MULT
                 )
 
-        def finish(g, terms):
-            recs = slice(g * REC, (g + 1) * REC)
-            z = psum.tile([P, PACK, REC], F32, name="tail", bufs=1)
+        def turn(bank, terms, which):
             for t in range(PACK):
-                for a in range(4):
+                for a in which:
                     nc.tensor.matmul(
-                        z[:, t, :], terms[:, a, t, :], identity[:], start=(a == 0), stop=(a == 3), is_transpose=True
+                        bank[:, t, :],
+                        terms[:, a, t, :],
+                        identity[:],
+                        start=(a == which[0]),
+                        stop=(a == which[-1]),
+                        is_transpose=True,
                     )
+            return bank[:].rearrange("p t v -> p v t")
+
+        def finish(g, terms, last):
+            recs = slice(g * REC, (g + 1) * REC)
             zm = work.tile([P, REC, PACK], BF16, name="zm", align_bytes=64)
-            nc.scalar.activation(zm[:], z[:].rearrange("p t v -> p v t"), COPY, scale=1.0 / 12.0)
+            if last:
+                z_first = psum.tile([P, PACK, REC], F32, name="e_even", bufs=1)
+                zm_first = work.tile([P, REC, PACK], F32, name="zm_first")
+                nc.scalar.activation(zm_first[:], turn(z_first, terms, [0, 1]), COPY, scale=1.0 / 12.0)
+                z = psum.tile([P, PACK, REC], F32, name="tail", bufs=1)
+                nc.vector.scalar_tensor_tensor(zm[:], turn(z, terms, [2, 3]), 1.0 / 12.0, zm_first[:], MULT, ADD)
+            else:
+                z = psum.tile([P, PACK, REC], F32, name="tail", bufs=1)
+                nc.scalar.activation(zm[:], turn(z, terms, [0, 1, 2, 3]), COPY, scale=1.0 / 12.0)
             zm_codes = work.tile([P, REC], U32, name="zm_codes", align_bytes=64)
             zm_plane = work.tile([P, REC], U8, name="zm_plane", align_bytes=64)
             nc.vector.quantize_mx(
@@ -189,17 +210,20 @@ def tile_picked_zfm_mean_po_kernel(
                     start=True,
                     stop=True,
                 )
-            y_out = work.tile([P, PACK, REC], F32, name="y_out")
-            nc.scalar.copy(y_out[:], y[:])
-            nc.sync.dma_start(out=out_0.rearrange("(p t) v -> p t v", t=PACK)[:, :, recs], in_=y_out[:])
             y_grouped = work.tile([P, REC, PACK], BF16, name="y_grouped", align_bytes=64)
-            nc.vector.tensor_copy(y_grouped[:], y_out[:].rearrange("p t v -> p v t"))
+            y_out = work.tile([P, PACK, REC], F32, name="y_out")
+            if last:
+                nc.vector.tensor_copy(y_grouped[:], y[:].rearrange("p t v -> p v t"))
+            else:
+                nc.scalar.copy(y_grouped[:], y[:].rearrange("p t v -> p v t"))
+            nc.scalar.copy(y_out[:], y[:])
             nc.vector.quantize_mx(
                 out=y_codes[:, recs].bitcast(FP8X4),
                 scales=y_plane[:, recs],
                 in_=y_grouped[:].rearrange("p v t -> p (v t)"),
             )
             nc.sync.dma_start(out=words_of(out_1)[:, recs], in_=y_codes[:, recs].bitcast(I32))
+            nc.scalar.dma_start(out=out_0.rearrange("(p t) v -> p t v", t=PACK)[:, :, recs], in_=y_out[:])
 
         terms = [work.tile([P, 4, PACK, P], F32, name="terms") for g in range(2)]
         quantise_w1(0)
@@ -208,10 +232,10 @@ def tile_picked_zfm_mean_po_kernel(
         block(0, 1, terms[0])
         load_w3()
         block(1, 0, terms[1])
-        finish(0, terms[0])
+        finish(0, terms[0], False)
         block(1, 1, terms[1])
-        finish(1, terms[1])
+        finish(1, terms[1], True)
         for q in range(4):
-            nc.scalar.dma_start(
+            nc.sync.dma_start(
                 out=out_2[0, 4 * q : 4 * q + 4, :].bitcast(I32), in_=y_plane[32 * q : 32 * q + 4, :].bitcast(I32)
             )

@@ -96,7 +96,7 @@ def tile_picked_zfm_mean_po_kernel(
         w1_codes, w1_plane = [], []
 
         def quantise_w1(ih):
-            grouped = keep.tile([P, HH * PACK], BF16, name="w1_grouped", align_bytes=64)
+            grouped = reuse.tile([P, HH * PACK], BF16, name=f"w1_grouped{ih}", align_bytes=64, offset=28672)
             nc.scalar.activation(
                 grouped[:].rearrange("p (m t j) -> p m j t", t=PACK, j=PACK),
                 w1_raw[ih][:].rearrange("p j (m t) -> p m j t", t=PACK),
@@ -108,10 +108,9 @@ def tile_picked_zfm_mean_po_kernel(
             w1_codes.append(codes)
             w1_plane.append(plane)
 
-        w3_codes = keep.tile([P, N], U32, name="w3_codes", align_bytes=64)
-        w3_plane = keep.tile([P, N], U8, name="w3_plane", align_bytes=64)
-
         def load_w3():
+            w3_codes = reuse.tile([P, N], U32, name="w3_codes", align_bytes=64, offset=28672 + 512)
+            w3_plane = reuse.tile([P, N], U8, name="w3_plane", align_bytes=64, offset=28672)
             raw = reuse.tile([P, N], U32, name="w3_raw", align_bytes=64, offset=24576)
             nc.sync.dma_start(out=raw[:].bitcast(I32), in_=words_of(w3_words))
             nc.gpsimd.tensor_copy(
@@ -123,6 +122,7 @@ def tile_picked_zfm_mean_po_kernel(
             nc.gpsimd.tensor_copy(
                 w3_plane[:].rearrange("p (t m) -> p t m", t=PACK), plane_raw[:].rearrange("p (m t) -> p t m", t=PACK)
             )
+            return w3_codes, w3_plane
 
         identity = reuse.tile([P, P], F32, name="identity", align_bytes=64, offset=20480)
         make_identity(nc, identity[:])
@@ -145,7 +145,7 @@ def tile_picked_zfm_mean_po_kernel(
         def dealt(bank):
             return bank[:].rearrange("p (a m t) -> p a t m", a=2, t=PACK)
 
-        def block(g, ih, terms):
+        def start_block(g, ih):
             cols = slice(ih * HH, (ih + 1) * HH)
             e_even = psum.tile([P, 2 * HH], F32, name="e_even", bufs=1)
             e_odd = psum.tile([P, 2 * HH], F32, name="e_odd", bufs=2)
@@ -155,19 +155,28 @@ def tile_picked_zfm_mean_po_kernel(
             project(e_odd, g, [[1], [3]], w2_codes[:, cols], w2_plane[W2_ROW:, cols])
             project(h_single, g, [[0], [2]], w1_codes[ih][:], w1_plane[ih][:])
             project(h_pair, g, [[2, 3], [0, 1]], w1_codes[ih][:], w1_plane[ih][:])
-
             even = work.tile([P, 2, PACK, MH], F32, name="even")
             nc.scalar.activation(even[:], dealt(e_even), COPY)
             even_sum = work.tile([P, 1, PACK, MH], F32, name="even_sum")
             nc.gpsimd.tensor_tensor(even_sum[:], even[:, 0:1], even[:, 1:2], ADD)
+            return e_odd, even, even_sum, h_single, h_pair
+
+        def difference(block):
+            e_odd, even = block[0], block[1]
             diff = work.tile([P, 2, PACK, MH], F32, name="diff")
             nc.vector.tensor_tensor(diff[:], dealt(e_odd), even[:], SUB)
+            return diff
+
+        def triple(block):
+            e_odd, even_sum = block[0], block[2]
             trio = work.tile([P, 2, PACK, MH], F32, name="trio")
             nc.vector.tensor_tensor(trio[:], dealt(e_odd), even_sum[:].to_broadcast([P, 2, PACK, MH]), ADD)
-            for a, (bank, factor) in enumerate(((h_single, diff), (h_pair, trio))):
-                nc.vector.tensor_tensor(
-                    terms[:, 2 * a : 2 * a + 2, :, ih * MH : (ih + 1) * MH], dealt(bank), factor[:], MULT
-                )
+            return trio
+
+        def multiply(terms, a, ih, bank, factor, ts=slice(0, PACK)):
+            nc.vector.tensor_tensor(
+                terms[:, 2 * a : 2 * a + 2, ts, ih * MH : (ih + 1) * MH], dealt(bank)[:, :, ts, :], factor[:, :, ts, :], MULT
+            )
 
         def turn(bank, terms, which):
             for t in range(PACK):
@@ -182,24 +191,27 @@ def tile_picked_zfm_mean_po_kernel(
                     )
             return bank[:].rearrange("p t v -> p v t")
 
-        def finish(g, terms, last):
-            recs = slice(g * REC, (g + 1) * REC)
+        def sum_terms(terms, last):
             zm = work.tile([P, REC, PACK], BF16, name="zm", align_bytes=64)
             if last:
                 z_first = psum.tile([P, PACK, REC], F32, name="e_even", bufs=1)
                 zm_first = work.tile([P, REC, PACK], F32, name="zm_first")
                 nc.scalar.activation(zm_first[:], turn(z_first, terms, [0, 1]), COPY, scale=1.0 / 12.0)
-                z = psum.tile([P, PACK, REC], F32, name="tail", bufs=1)
+                z = psum.tile([P, PACK, REC], F32, name="e_odd", bufs=2)
                 nc.vector.scalar_tensor_tensor(zm[:], turn(z, terms, [2, 3]), 1.0 / 12.0, zm_first[:], MULT, ADD)
             else:
                 z = psum.tile([P, PACK, REC], F32, name="tail", bufs=1)
                 nc.scalar.activation(zm[:], turn(z, terms, [0, 1, 2, 3]), COPY, scale=1.0 / 12.0)
+            return zm
+
+        def finish(g, zm, last):
+            recs = slice(g * REC, (g + 1) * REC)
             zm_codes = work.tile([P, REC], U32, name="zm_codes", align_bytes=64)
             zm_plane = work.tile([P, REC], U8, name="zm_plane", align_bytes=64)
             nc.vector.quantize_mx(
                 out=zm_codes[:].bitcast(FP8X4), scales=zm_plane[:], in_=zm[:].rearrange("p v t -> p (v t)")
             )
-            y = psum.tile([P, PACK, REC], F32, name="tail", bufs=1)
+            y = psum.tile([P, PACK, REC], F32, name="h_single" if last else "tail", bufs=2 if last else 1)
             for t in range(PACK):
                 nc.tensor.matmul_mx(
                     out=y[:, t, :],
@@ -212,30 +224,44 @@ def tile_picked_zfm_mean_po_kernel(
                 )
             y_grouped = work.tile([P, REC, PACK], BF16, name="y_grouped", align_bytes=64)
             y_out = work.tile([P, PACK, REC], F32, name="y_out")
+            nc.scalar.copy(y_out[:], y[:])
+            nc.scalar.dma_start(out=out_0.rearrange("(p t) v -> p t v", t=PACK)[:, :, recs], in_=y_out[:])
             if last:
-                nc.vector.tensor_copy(y_grouped[:], y[:].rearrange("p t v -> p v t"))
+                nc.vector.tensor_copy(
+                    y_grouped[:].rearrange("p (c i) t -> p c t i", i=4), y_out[:].rearrange("p t (c i) -> p c t i", i=4)
+                )
             else:
                 nc.scalar.copy(y_grouped[:], y[:].rearrange("p t v -> p v t"))
-            nc.scalar.copy(y_out[:], y[:])
             nc.vector.quantize_mx(
                 out=y_codes[:, recs].bitcast(FP8X4),
                 scales=y_plane[:, recs],
                 in_=y_grouped[:].rearrange("p v t -> p (v t)"),
             )
             nc.sync.dma_start(out=words_of(out_1)[:, recs], in_=y_codes[:, recs].bitcast(I32))
-            nc.scalar.dma_start(out=out_0.rearrange("(p t) v -> p t v", t=PACK)[:, :, recs], in_=y_out[:])
 
         terms = [work.tile([P, 4, PACK, P], F32, name="terms") for g in range(2)]
-        quantise_w1(0)
-        block(0, 0, terms[0])
-        quantise_w1(1)
-        block(0, 1, terms[0])
-        load_w3()
-        block(1, 0, terms[1])
-        finish(0, terms[0], False)
-        block(1, 1, terms[1])
-        finish(1, terms[1], True)
+        for ih in range(2):
+            quantise_w1(ih)
+            block = start_block(0, ih)
+            diff, trio = difference(block), triple(block)
+            multiply(terms[0], 0, ih, block[3], diff)
+            multiply(terms[0], 1, ih, block[4], trio)
+        low = start_block(1, 0)
+        diff_low, trio_low = difference(low), triple(low)
+        high = start_block(1, 1)
+        w3_codes, w3_plane = load_w3()
+        zm_first_half = sum_terms(terms[0], False)
+        diff_high = difference(high)
+        multiply(terms[1], 0, 0, low[3], diff_low)
+        multiply(terms[1], 0, 1, high[3], diff_high)
+        trio_high = triple(high)
+        for ts in (slice(0, 2), slice(2, 4)):
+            multiply(terms[1], 1, 0, low[4], trio_low, ts)
+            multiply(terms[1], 1, 1, high[4], trio_high, ts)
+        zm_second_half = sum_terms(terms[1], True)
+        finish(0, zm_first_half, False)
+        finish(1, zm_second_half, True)
         for q in range(4):
-            nc.sync.dma_start(
+            [nc.sync, nc.scalar][q % 2].dma_start(
                 out=out_2[0, 4 * q : 4 * q + 4, :].bitcast(I32), in_=y_plane[32 * q : 32 * q + 4, :].bitcast(I32)
             )

@@ -85,13 +85,22 @@ def tile_picked_zfm_mean_po_kernel(
         w1_raw.append(load_w1(1, 16384))
 
         x_codes = []
-        for g in range(2):
-            codes = keep.tile([P, D, REC], U32, name=f"x_codes{g}", align_bytes=64)
+
+        def pick_words(g):
+            picked = keep.tile([P, REC * D], U32, name="x_picked", align_bytes=64)
             cols = REC * D // 16
+            nc.vector.tensor_copy(picked[:], x_table[:].indirect(offsets[:, g * cols : (g + 1) * cols]))
+            return picked
+
+        def sort_words(g, picked):
+            codes = keep.tile([P, D, REC], U32, name=f"x_codes{g}", align_bytes=64)
             nc.vector.tensor_copy(
-                codes[:].rearrange("p d v -> p v d"), x_table[:].indirect(offsets[:, g * cols : (g + 1) * cols])
+                codes[:].rearrange("p d (c i) -> p c d i", i=4), picked[:].rearrange("p (c i d) -> p c d i", i=4, d=D)
             )
             x_codes.append(codes)
+
+        sort_words(0, pick_words(0))
+        picked_second = pick_words(1)
 
         w1_codes, w1_plane = [], []
 
@@ -242,6 +251,8 @@ def tile_picked_zfm_mean_po_kernel(
         terms = [work.tile([P, 4, PACK, P], F32, name="terms") for g in range(2)]
         for ih in range(2):
             quantise_w1(ih)
+            if ih == 0:
+                sort_words(1, picked_second)
             block = start_block(0, ih)
             diff, trio = difference(block), triple(block)
             multiply(terms[0], 0, ih, block[3], diff)

from contextlib import ExitStack

import concourse.mybir as mybir
from concourse.masks import make_identity

K, T, S, D, V, H, N = 512, 4096, 1024, 4, 256, 512, 512
FLOPS = 2 * (2 * K * H * S) + 2 * H * N * V

F32 = mybir.dt.float32
BF16 = mybir.dt.bfloat16
I32 = mybir.dt.int32
U32 = mybir.dt.uint32
U16 = mybir.dt.uint16
U8 = mybir.dt.uint8
FP8X4 = mybir.dt.float8_e4m3fn_x4
ADD = mybir.AluOpType.add
SUB = mybir.AluOpType.subtract
MULT = mybir.AluOpType.mult
COPY = mybir.ActivationFunctionType.Copy

P = 128
PACK = 4
REC = 128
HH = H // 2
MH = HH // PACK
W2_ROW = 4
W3_ROW = 8


def load_scale_rows(queues, plane, scales, first_row):
    for q in range(4):
        queues[q % len(queues)].dma_start(
            out=plane[32 * q + first_row : 32 * q + first_row + 4, :].bitcast(I32),
            in_=scales[0, 4 * q : 4 * q + 4, :].bitcast(I32),
        )


def words_of(dram):
    return dram[0].rearrange("p n t -> p (n t)").bitcast(I32)


def tile_picked_zfm_mean_po_kernel(
    tc, x_words, x_scales, w1, w2_words, w2_scales, w3_words, w3_scales, offs, out_0, out_1, out_2
):
    nc = tc.nc
    with ExitStack() as ctx:
        keep = ctx.enter_context(tc.tile_pool(name="keep", bufs=1))
        reuse = ctx.enter_context(tc.tile_pool(name="reuse", bufs=1))
        work = ctx.enter_context(tc.tile_pool(name="work", bufs=2))
        psum = ctx.enter_context(tc.psum_pool(name="psum", bufs=1))

        xs_table = keep.tile([P, T], U8, name="xs_table", align_bytes=64)
        nc.sync.dma_start(out=xs_table[P - 16 :, :].bitcast(I32), in_=x_scales[0].bitcast(I32))
        nc.vector.memset(xs_table[: P - 16, :].bitcast(I32), 0)
        offsets = keep.tile([P, S // 16], U16, name="offsets")
        nc.sync.dma_start(offsets[:], offs)
        x_table = reuse.tile([P, T], U32, name="x_table", align_bytes=64, offset=0)
        nc.sync.dma_start(out=x_table[:].bitcast(I32), in_=words_of(x_words))

        def load_w1(ih, offset):
            raw = reuse.tile([P, PACK, HH], F32, name=f"w1_raw{ih}", align_bytes=64, offset=offset)
            nc.sync.dma_start(out=raw[:], in_=w1[:, ih * HH : (ih + 1) * HH].rearrange("(p j) c -> p j c", j=PACK))
            return raw

        w1_raw = [load_w1(0, 24576)]
        w2_codes = keep.tile([P, H], U32, name="w2_codes", align_bytes=64)
        nc.sync.dma_start(out=w2_codes[:].bitcast(I32), in_=words_of(w2_words))


        w2_plane = keep.tile([P, H], U8, name="w2_plane", align_bytes=64)
        nc.gpsimd.memset(w2_plane[:].bitcast(I32), 0)
        load_scale_rows([nc.gpsimd], w2_plane, w2_scales, W2_ROW)

        xs_picked = reuse.tile([P, S], U8, name="xs_picked", align_bytes=64, offset=20480 - 512)
        nc.vector.tensor_copy(xs_picked[:], xs_table[:].indirect(offsets[:]))
        xs_sorted = keep.tile([P, 2, D, REC], U8, name="xs_sorted", align_bytes=64)
        nc.vector.tensor_copy(xs_sorted[:], xs_picked[:].rearrange("p (g v d) -> p g d v", g=2, d=D))
        x_plane = keep.tile([P, 2, D, REC], U8, name="x_plane", align_bytes=64)
        nc.vector.memset(x_plane[:].bitcast(I32), 0)
        for q in range(4):
            nc.sync.dma_start(
                out=x_plane[32 * q : 32 * q + 4].rearrange("p g d v -> p (g d v)").bitcast(I32),
                in_=xs_sorted[P - 16 + 4 * q : P - 12 + 4 * q].rearrange("p g d v -> p (g d v)").bitcast(I32),
            )
        w1_raw.append(load_w1(1, 16384))

        x_codes = []

        def pick_words(g):
            picked = keep.tile([P, REC * D], U32, name="x_picked", align_bytes=64)
            cols = REC * D // 16
            nc.vector.tensor_copy(picked[:], x_table[:].indirect(offsets[:, g * cols : (g + 1) * cols]))
            return picked

        def sort_words(g, picked):
            codes = keep.tile([P, D, REC], U32, name=f"x_codes{g}", align_bytes=64)
            nc.vector.tensor_copy(
                codes[:].rearrange("p d (c i) -> p c d i", i=4), picked[:].rearrange("p (c i d) -> p c d i", i=4, d=D)
            )
            x_codes.append(codes)

        sort_words(0, pick_words(0))
        picked_second = pick_words(1)

        w1_codes, w1_plane = [], []

        def quantise_w1(ih):
            grouped = reuse.tile([P, HH * PACK], BF16, name=f"w1_grouped{ih}", align_bytes=64, offset=28672)
            nc.scalar.activation(
                grouped[:].rearrange("p (m t j) -> p m j t", t=PACK, j=PACK),
                w1_raw[ih][:].rearrange("p j (m t) -> p m j t", t=PACK),
                COPY,
            )
            codes = reuse.tile([P, HH], U32, name=f"w1_codes{ih}", align_bytes=64, offset=1024 * ih)
            plane = keep.tile([P, HH], U8, name=f"w1_plane{ih}", align_bytes=64)
            nc.vector.quantize_mx(out=codes[:].bitcast(FP8X4), scales=plane[:], in_=grouped[:])
            w1_codes.append(codes)
            w1_plane.append(plane)

        def load_w3():
            w3_codes = reuse.tile([P, N], U32, name="w3_codes", align_bytes=64, offset=28672 + 512)
            w3_plane = reuse.tile([P, N], U8, name="w3_plane", align_bytes=64, offset=28672)
            raw = reuse.tile([P, N], U32, name="w3_raw", align_bytes=64, offset=24576)
            nc.sync.dma_start(out=raw[:].bitcast(I32), in_=words_of(w3_words))
            nc.gpsimd.tensor_copy(
                w3_codes[:].rearrange("p (t m) -> p t m", t=PACK), raw[:].rearrange("p (m t) -> p t m", t=PACK)
            )
            plane_raw = reuse.tile([P, N], U8, name="w3_plane_raw", align_bytes=64, offset=2048)
            nc.gpsimd.memset(plane_raw[:].bitcast(I32), 0)
            load_scale_rows([nc.sync], plane_raw, w3_scales, W3_ROW)
            nc.gpsimd.tensor_copy(
                w3_plane[:].rearrange("p (t m) -> p t m", t=PACK), plane_raw[:].rearrange("p (m t) -> p t m", t=PACK)
            )
            return w3_codes, w3_plane

        identity = reuse.tile([P, P], F32, name="identity", align_bytes=64, offset=20480)
        make_identity(nc, identity[:])
        y_codes = keep.tile([P, V], U32, name="y_codes", align_bytes=64)
        y_plane = keep.tile([P, V], U8, name="y_plane", align_bytes=64)

        def project(bank, g, fields, codes, plane):
            for a, group in enumerate(fields):
                for n, d in enumerate(group):
                    nc.tensor.matmul_mx(
                        out=bank[:, a * HH : (a + 1) * HH],
                        lhsT=x_codes[g][:, d, :].bitcast(FP8X4),
                        lhsT_scale=x_plane[:, g, d, :],
                        rhs=codes.bitcast(FP8X4),
                        rhs_scale=plane,
                        start=(n == 0),
                        stop=(n == len(group) - 1),
                    )

        def dealt(bank):
            return bank[:].rearrange("p (a m t) -> p a t m", a=2, t=PACK)

        def start_block(g, ih):
            cols = slice(ih * HH, (ih + 1) * HH)
            e_even = psum.tile([P, 2 * HH], F32, name="e_even", bufs=1)
            e_odd = psum.tile([P, 2 * HH], F32, name="e_odd", bufs=2)
            h_single = psum.tile([P, 2 * HH], F32, name="h_single", bufs=2)
            h_pair = psum.tile([P, 2 * HH], F32, name="h_pair", bufs=2)
            project(e_even, g, [[0], [2]], w2_codes[:, cols], w2_plane[W2_ROW:, cols])
            project(e_odd, g, [[1], [3]], w2_codes[:, cols], w2_plane[W2_ROW:, cols])
            project(h_single, g, [[0], [2]], w1_codes[ih][:], w1_plane[ih][:])
            project(h_pair, g, [[2, 3], [0, 1]], w1_codes[ih][:], w1_plane[ih][:])
            even = work.tile([P, 2, PACK, MH], F32, name="even")
            nc.scalar.activation(even[:], dealt(e_even), COPY)
            even_sum = work.tile([P, 1, PACK, MH], F32, name="even_sum")
            nc.gpsimd.tensor_tensor(even_sum[:], even[:, 0:1], even[:, 1:2], ADD)
            return e_odd, even, even_sum, h_single, h_pair

        def difference(block):
            e_odd, even = block[0], block[1]
            diff = work.tile([P, 2, PACK, MH], F32, name="diff")
            nc.vector.tensor_tensor(diff[:], dealt(e_odd), even[:], SUB)
            return diff

        def triple(block):
            e_odd, even_sum = block[0], block[2]
            trio = work.tile([P, 2, PACK, MH], F32, name="trio")
            nc.vector.tensor_tensor(trio[:], dealt(e_odd), even_sum[:].to_broadcast([P, 2, PACK, MH]), ADD)
            return trio

        def multiply(terms, a, ih, bank, factor, ts=slice(0, PACK)):
            nc.vector.tensor_tensor(
                terms[:, 2 * a : 2 * a + 2, ts, ih * MH : (ih + 1) * MH], dealt(bank)[:, :, ts, :], factor[:, :, ts, :], MULT
            )

        def turn(bank, terms, which):
            for t in range(PACK):
                for a in which:
                    nc.tensor.matmul(
                        bank[:, t, :],
                        terms[:, a, t, :],
                        identity[:],
                        start=(a == which[0]),
                        stop=(a == which[-1]),
                        is_transpose=True,
                    )
            return bank[:].rearrange("p t v -> p v t")

        def sum_terms(terms, last):
            zm = work.tile([P, REC, PACK], BF16, name="zm", align_bytes=64)
            if last:
                z_first = psum.tile([P, PACK, REC], F32, name="e_even", bufs=1)
                zm_first = work.tile([P, REC, PACK], F32, name="zm_first")
                nc.scalar.activation(zm_first[:], turn(z_first, terms, [0, 1]), COPY, scale=1.0 / 12.0)
                z = psum.tile([P, PACK, REC], F32, name="e_odd", bufs=2)
                nc.vector.scalar_tensor_tensor(zm[:], turn(z, terms, [2, 3]), 1.0 / 12.0, zm_first[:], MULT, ADD)
            else:
                z = psum.tile([P, PACK, REC], F32, name="tail", bufs=1)
                nc.scalar.activation(zm[:], turn(z, terms, [0, 1, 2, 3]), COPY, scale=1.0 / 12.0)
            return zm

        def finish(g, zm, last):
            recs = slice(g * REC, (g + 1) * REC)
            zm_codes = work.tile([P, REC], U32, name="zm_codes", align_bytes=64)
            zm_plane = work.tile([P, REC], U8, name="zm_plane", align_bytes=64)
            nc.vector.quantize_mx(
                out=zm_codes[:].bitcast(FP8X4), scales=zm_plane[:], in_=zm[:].rearrange("p v t -> p (v t)")
            )
            y = psum.tile([P, PACK, REC], F32, name="h_single" if last else "tail", bufs=2 if last else 1)
            for t in range(PACK):
                nc.tensor.matmul_mx(
                    out=y[:, t, :],
                    lhsT=w3_codes[:, t * P : (t + 1) * P].bitcast(FP8X4),
                    lhsT_scale=w3_plane[W3_ROW:, t * P : (t + 1) * P],
                    rhs=zm_codes[:].bitcast(FP8X4),
                    rhs_scale=zm_plane[:],
                    start=True,
                    stop=True,
                )
            y_grouped = work.tile([P, REC, PACK], BF16, name="y_grouped", align_bytes=64)
            y_out = work.tile([P, PACK, REC], F32, name="y_out")
            nc.scalar.copy(y_out[:], y[:])
            nc.scalar.dma_start(out=out_0.rearrange("(p t) v -> p t v", t=PACK)[:, :, recs], in_=y_out[:])
            if last:
                nc.vector.tensor_copy(
                    y_grouped[:].rearrange("p (c i) t -> p c t i", i=4), y_out[:].rearrange("p t (c i) -> p c t i", i=4)
                )
            else:
                nc.scalar.copy(y_grouped[:], y[:].rearrange("p t v -> p v t"))
            nc.vector.quantize_mx(
                out=y_codes[:, recs].bitcast(FP8X4),
                scales=y_plane[:, recs],
                in_=y_grouped[:].rearrange("p v t -> p (v t)"),
            )
            nc.sync.dma_start(out=words_of(out_1)[:, recs], in_=y_codes[:, recs].bitcast(I32))

        terms = [work.tile([P, 4, PACK, P], F32, name="terms") for g in range(2)]
        for ih in range(2):
            quantise_w1(ih)
            if ih == 0:
                sort_words(1, picked_second)
            block = start_block(0, ih)
            diff, trio = difference(block), triple(block)
            multiply(terms[0], 0, ih, block[3], diff)
            multiply(terms[0], 1, ih, block[4], trio)
        low = start_block(1, 0)
        diff_low, trio_low = difference(low), triple(low)
        high = start_block(1, 1)
        w3_codes, w3_plane = load_w3()
        zm_first_half = sum_terms(terms[0], False)
        diff_high = difference(high)
        multiply(terms[1], 0, 0, low[3], diff_low)
        multiply(terms[1], 0, 1, high[3], diff_high)
        trio_high = triple(high)
        for ts in (slice(0, 2), slice(2, 4)):
            multiply(terms[1], 1, 0, low[4], trio_low, ts)
            multiply(terms[1], 1, 1, high[4], trio_high, ts)
        zm_second_half = sum_terms(terms[1], True)
        finish(0, zm_first_half, False)
        finish(1, zm_second_half, True)
        for q in range(4):
            [nc.sync, nc.scalar][q % 2].dma_start(
                out=out_2[0, 4 * q : 4 * q + 4, :].bitcast(I32), in_=y_plane[32 * q : 32 * q + 4, :].bitcast(I32)
            )
